import numpy as np
import ml_dtypes


def mxq(x, axis, fmt="e4m3"):
    dtype, down = {"e4m3": (ml_dtypes.float8_e4m3fn, 7), "e5m2": (ml_dtypes.float8_e5m2, 14)}[fmt]
    v = np.moveaxis(np.asarray(x, np.float32).astype(ml_dtypes.bfloat16).astype(np.float64), axis, -1)
    blocks = v.reshape(v.shape[:-1] + (-1, 32))
    amax = np.abs(blocks).max(-1, keepdims=True)
    byte = np.maximum(np.where(amax > 0, np.frexp(amax)[1] - 1 + 127, 0) - down, 1)
    scale = np.exp2(byte - 127.0)
    codes = (blocks / scale).astype(np.float32).astype(dtype).astype(np.float64)
    return np.moveaxis((codes * scale).reshape(v.shape), -1, axis)


WIDE = False


def mx_kscale(k):
    if not WIDE:
        return np.ones(k)
    levels = np.array([10, -10, 5, -5, 0])
    if k % 512:
        return np.exp2(np.random.permutation(np.resize(levels, k // 32))).repeat(32)
    a = np.empty((k // 512, 16))
    for p in range(k // 512):
        a[p, :8] = np.random.permutation(np.resize(levels, 8))
        for g in range(8):
            far = levels[np.abs(levels - a[p, g]) >= 10]
            a[p, g + 8] = far[np.random.randint(len(far))]
    return np.exp2(a.ravel()).repeat(32)


BF16 = ml_dtypes.bfloat16


def bf(x):
    return np.asarray(x, np.float32).astype(BF16)


def f64(x):
    return np.asarray(x).astype(np.float64)


B, P, S, K, C = 2, 1024, 512, 1024, 512


def instance_norm(x):
    mu = np.mean(x, axis=1, keepdims=True)
    centered = x - mu
    var = np.mean(centered * centered, axis=1, keepdims=True)
    return centered / np.sqrt(var + 1e-5)


def draw0():
    s, t = mx_kscale(S), mx_kscale(K)
    return {
        "x": bf(0.5 + 1.5 * np.random.standard_normal((B, P, C))),
        "m": bf(np.random.standard_normal((B, P, S)) * s),
        "wm": bf(np.random.standard_normal((S, K)) / np.sqrt(S) / s[:, None]),
        "bm": bf(0.3 * np.random.standard_normal(K)),
        "g": bf(np.random.standard_normal(K) * t),
        "wg": bf(np.random.standard_normal((K, C)) / np.sqrt(K) / t[:, None]),
        "wb": bf(np.random.standard_normal((K, C)) / np.sqrt(K) / t[:, None]),
    }


def core(x, m, wm, bm, g, wg, wb):
    h = (mxq(f64(m), 2, "e4m3") @ mxq(f64(wm), 0, "e4m3")) + f64(bm)[None, None, :]
    a = np.maximum(h, 0.0) * f64(g)[None, None, :]
    aq = mxq(a, 2, "e4m3")
    gamma = aq @ mxq(f64(wg), 0, "e4m3")
    beta = aq @ mxq(f64(wb), 0, "e4m3")
    xn = instance_norm(f64(x))
    y = xn * (1.0 + gamma) + beta
    return np.where(y >= 0.0, y, 0.2 * y)


def e4m3fn_bytes(y):
    return np.clip(np.asarray(y, np.float64), -448.0, 448.0).astype(np.float32).astype(ml_dtypes.float8_e4m3fn).view(np.uint8)


def e4m3fn_values(b):
    return np.asarray(b, np.uint8).view(ml_dtypes.float8_e4m3fn).astype(np.float64)


def setup_inputs():
    d = draw0()
    x0 = np.asarray(d['m']).astype(np.float64)
    s = (np.max(np.abs(x0), axis=(0, 1), keepdims=True) / 448.0).astype(np.float32)
    out = {}
    for k, v in d.items():
        if k == 'm':
            out['m_bytes'] = e4m3fn_bytes(x0 / s.astype(np.float64))
            out['m_scale'] = s
        else:
            out[k] = v
    return out


def reference(x, m_bytes, m_scale, wm, bm, g, wg, wb):
    return core(x, e4m3fn_values(m_bytes) * m_scale.astype(np.float64), wm, bm, g, wg, wb)

@@ -1,0 +1,421 @@
+from contextlib import ExitStack
+
+import concourse.mybir as mybir
+from concourse.masks import make_identity
+
+B, P, S, K, C = 2, 1024, 512, 1024, 512
+FLOPS = 2 * B * P * S * K + 2 * 2 * B * P * K * C
+
+F32 = mybir.dt.float32
+BF16 = mybir.dt.bfloat16
+U32 = mybir.dt.uint32
+U8 = mybir.dt.uint8
+FP8 = mybir.dt.float8_e4m3fn
+FP8X4 = mybir.dt.float8_e4m3fn_x4
+ACT = mybir.ActivationFunctionType
+ALU = mybir.AluOpType
+
+TI = 8
+T_BANKS = 1
+H_BANKS = 3
+S_BANKS = 4
+GRP = 512
+A_ON_VECTOR = ()
+W_ON_SCALAR = ((0, 1), (1, 1))
+LEAKY_ON_GPSIMD = ((0, 0), (0, 1), (1, 0), (1, 1), (2, 0), (2, 1))
+SIGN_ON_GPSIMD = True
+
+
+def tile_spademodulationpointwise_kernel(tc, x, m_bytes, m_scale, wm, bm, g, wg, wb, out):
+    nc = tc.nc
+    with ExitStack() as ctx:
+        keep = ctx.enter_context(tc.tile_pool(name="keep", bufs=1))
+        work = ctx.enter_context(tc.tile_pool(name="work", bufs=3))
+        psum = ctx.enter_context(tc.psum_pool(name="psum", bufs=2))
+
+        sc = keep.tile([128, S], F32, name="sc")
+        nc.scalar.dma_start(out=sc[:], in_=m_scale.rearrange("o q k -> (o q k)").partition_broadcast(128))
+        gv = keep.tile([128, 8], BF16, name="gv")
+        bv = keep.tile([128, 8], BF16, name="bv")
+        nc.scalar.dma_start(out=gv[:].rearrange("p (h t) -> p h t", t=4), in_=g.rearrange("(h p t) -> p h t", p=128, t=4))
+        nc.scalar.dma_start(out=bv[:].rearrange("p (h t) -> p h t", t=4), in_=bm.rearrange("(h p t) -> p h t", p=128, t=4))
+
+        mb = [keep.tile([128, 4, S], U8, name=f"mb{q}", align_bytes=64) for q in range(4)]
+        wr = [keep.tile([128, 4, 512], BF16, name=f"wr{h}", align_bytes=64) for h in range(2)]
+        xt = [keep.tile([128, 4, C], BF16, name=f"xt{q}", align_bytes=64) for q in range(4)]
+        vr = [keep.tile([128, 2, 4, C], BF16, name=f"vr{h}", align_bytes=64) for h in range(2)]
+        wm_v = wm.rearrange("(p j) n -> p j n", j=4)
+
+        def load_m(q):
+            b, h = divmod(q, 2)
+            nc.sync.dma_start(out=mb[q][:], in_=m_bytes[b].rearrange("(p i) k -> p i k", i=TI)[:, 4 * h : 4 * h + 4, :])
+
+        def load_x(q):
+            b, h = divmod(q, 2)
+            nc.sync.dma_start(out=xt[q][:], in_=x[b].rearrange("(p i) c -> p i c", i=TI)[:, 4 * h : 4 * h + 4, :])
+
+        load_m(0)
+        nc.sync.dma_start(out=wr[0][:], in_=wm_v[:, :, 0:512])
+        nc.sync.dma_start(out=wr[1][:], in_=wm_v[:, :, 512:1024])
+        load_m(1)
+        for w, src in enumerate((wg, wb)):
+            for h in range(2):
+                nc.sync.dma_start(out=vr[h][:, w], in_=src[512 * h : 512 * h + 512, :].rearrange("(p j) c -> p j c", j=4))
+        load_x(0)
+        load_x(1)
+        load_m(2)
+        load_m(3)
+        load_x(2)
+        load_x(3)
+
+        hold = {}
+
+        idf = keep.tile([128, 128], F32, name="idf")
+        make_identity(nc, idf[:])
+        idb = keep.tile([128, 128], BF16, name="idb")
+        make_identity(nc, idb[:])
+        sel_r = keep.tile([128, 128], BF16, name="sel_r")
+        sel_m = keep.tile([128, 128], BF16, name="sel_m")
+        nc.gpsimd.memset(sel_r[:], 0.0)
+        nc.gpsimd.memset(sel_r[0:3, :], 1.0)
+        nc.gpsimd.memset(sel_m[:], 0.0)
+        nc.gpsimd.memset(sel_m[32:35, :], 1.0)
+        rs = [keep.tile([128, 4, 128], BF16, name=f"rs{b}") for b in range(2)]
+        for b in range(2):
+            nc.gpsimd.memset(rs[b][:], 0.0)
+
+        ng = keep.tile([128, 8], F32, name="ng")
+        ag = keep.tile([128, 8], F32, name="ag")
+        gb = keep.tile([128, 8], F32, name="gb")
+        sg0 = keep.tile([128, 8], F32, name="sg0")
+        sg = keep.tile([128, 8], F32, name="sg")
+        nc.vector.tensor_scalar(out=ng[:], in0=gv[:], scalar1=-1.0, scalar2=None, op0=ALU.mult)
+        nc.vector.tensor_scalar(out=sg0[:], in0=gv[:], scalar1=0.0, scalar2=2.0, op0=ALU.is_ge, op1=ALU.mult)
+        nc.vector.tensor_tensor(out=ag[:], in0=gv[:], in1=ng[:], op=ALU.max)
+        nc.vector.tensor_scalar(out=sg[:], in0=sg0[:], scalar1=-1.0, scalar2=None, op0=ALU.add)
+        nc.vector.tensor_tensor(out=gb[:], in0=ag[:], in1=bv[:], op=ALU.mult)
+
+        mq = keep.tile([128, 2048], U32, name="mq", align_bytes=64)
+        ms = keep.tile([128, 2048], U8, name="ms", align_bytes=64)
+        wq = keep.tile([128, 1024], U32, name="wq", align_bytes=64)
+        ws = keep.tile([128, 1024], U8, name="ws", align_bytes=64)
+        vq = keep.tile([128, 2, 2, 512], U32, name="vq", align_bytes=64)
+        vs = keep.tile([128, 2, 2, 512], U8, name="vs", align_bytes=64)
+        st = keep.tile([128, 2, 4, 2, 6], F32, name="st")
+        mv = keep.tile([128, 2, 4, 2], F32, name="mv")
+        rb = [keep.tile([128, C], F32, name=f"rb{b}") for b in range(2)]
+        rows = [keep.tile([128, C], BF16, name=f"rows{b}") for b in range(2)]
+
+        def interleave(on_vector, dst, src):
+            o = dst.rearrange("p (c i) t -> p c t i", i=4)
+            s = src.rearrange("p t (c i) -> p c t i", i=4)
+            if on_vector:
+                nc.vector.tensor_copy(out=o, in_=s)
+            else:
+                nc.scalar.copy(out=o, in_=s)
+
+        def m_product(q, pair):
+            bank = psum.tile([128, 2, 2, 128], F32, tag="t", name="mt", bufs=T_BANKS)
+            hold["t", q, pair] = bank
+            for il in range(2):
+                mp = work.tile([128, S], BF16, tag="mp", name="mp", align_bytes=64, bufs=4)
+                nc.vector.tensor_tensor(out=mp[:], in0=mb[q][:, 2 * pair + il, :].bitcast(FP8), in1=sc[:], op=ALU.mult)
+                w = mp[:].bitcast(F32)
+                for u in range(2):
+                    nc.tensor.transpose(bank[:, il, u, :], w[:, u : 256 : 2], idf[:])
+
+        def m_out(q, pair):
+            if pair == 0:
+                hold["mg", q] = work.tile([128, GRP, 4], BF16, tag="mg", name="mg", align_bytes=64, bufs=2)
+            mgw = hold["mg", q][:].rearrange("p n t -> p (n t)").bitcast(F32)
+            nc.scalar.copy(
+                out=mgw[:, 512 * pair : 512 * pair + 512].rearrange("p (i r u) -> p i r u", i=2, u=2),
+                in_=hold["t", q, pair][:].rearrange("p i u r -> p i r u"),
+            )
+
+        def m_quant(q):
+            nc.vector.quantize_mx(
+                out=mq[:, GRP * q : GRP * q + GRP].bitcast(FP8X4),
+                scales=ms[:, GRP * q : GRP * q + GRP],
+                in_=hold["mg", q][:].rearrange("p n t -> p (n t)"),
+            )
+
+        def wm_inter(h):
+            wgr = work.tile([128, 4, 128, 4], BF16, tag="wgr", name="wgr", align_bytes=64, bufs=2)
+            hold["wgr", h] = wgr
+            nc.vector.tensor_copy(out=wgr[:], in_=wr[h][:].rearrange("p j (m t) -> p t m j", t=4))
+
+        def wm_quant(h):
+            nc.vector.quantize_mx(
+                out=wq[:, 512 * h : 512 * h + 512].bitcast(FP8X4),
+                scales=ws[:, 512 * h : 512 * h + 512],
+                in_=hold["wgr", h][:].rearrange("p t m j -> p (t m j)"),
+            )
+
+        def w_sign(h, w):
+            for j in range(4):
+                k = 4 * h + j
+                if SIGN_ON_GPSIMD:
+                    nc.gpsimd.tensor_scalar(out=vr[h][:, w, j, :], in0=vr[h][:, w, j, :], scalar1=sg[:, k : k + 1], scalar2=0.0, op0=ALU.mult, op1=ALU.add)
+                else:
+                    nc.vector.tensor_scalar(out=vr[h][:, w, j, :], in0=vr[h][:, w, j, :], scalar1=sg[:, k : k + 1], scalar2=None, op0=ALU.mult)
+
+        def w_inter(h, w):
+            vg = work.tile([128, C, 4], BF16, tag="vg", name="vg", align_bytes=64, bufs=3)
+            hold["vg", h, w] = vg
+            interleave(("vi", h, w) in vector_list, vg[:], vr[h][:, w])
+
+        def w_quant(h, w):
+            nc.vector.quantize_mx(
+                out=vq[:, h, w, :].bitcast(FP8X4), scales=vs[:, h, w, :], in_=hold["vg", h, w][:].rearrange("p c t -> p (c t)")
+            )
+
+        def x_aggr(b):
+            for cb in range(4):
+                nc.vector.bn_aggr(out=mv[:, b, cb, :], in_=st[:, b, cb].rearrange("p h s -> p (h s)"))
+            for name in ("ve", "sd"):
+                hold[name, b] = keep.tile([128, 4], F32, name=f"{name}{b}")
+            for name in ("rm", "r1", "r2"):
+                hold[name, b] = keep.tile([128, 4, 2], F32, name=f"{name}{b}")
+            nc.vector.tensor_scalar(out=hold["ve", b][:], in0=mv[:, b, :, 1], scalar1=1e-5, scalar2=None, op0=ALU.add)
+            nc.vector.tensor_scalar(out=hold["rm", b][:, :, 1], in0=mv[:, b, :, 0], scalar1=-1.0, scalar2=None, op0=ALU.mult)
+
+        def x_sqrt(b):
+            nc.scalar.activation(out=hold["sd", b][:], in_=hold["ve", b][:], func=ACT.Sqrt)
+
+        def x_split(b):
+            rm, r1, r2 = hold["rm", b], hold["r1", b], hold["r2", b]
+            nc.vector.reciprocal(out=rm[:, :, 0], in_=hold["sd", b][:])
+            nc.gpsimd.tensor_copy(out=rs[b][:, :, 0:64:32], in_=rm[:])
+            nc.gpsimd.tensor_tensor(out=r1[:], in0=rm[:], in1=rs[b][:, :, 0:64:32], op=ALU.subtract)
+            nc.gpsimd.tensor_copy(out=rs[b][:, :, 1:64:32], in_=r1[:])
+            nc.gpsimd.tensor_tensor(out=r2[:], in0=r1[:], in1=rs[b][:, :, 1:64:32], op=ALU.subtract)
+            nc.gpsimd.tensor_copy(out=rs[b][:, :, 2:64:32], in_=r2[:])
+
+        def rows_turn(b):
+            rp = psum.tile([128, 4, 128], BF16, tag="s", name="rp", bufs=S_BANKS)
+            hold["rp", b] = rp
+            for cb in range(4):
+                nc.tensor.transpose(rp[:, cb, :], rs[b][:, cb, :], idb[:])
+
+        def rows_out(b):
+            nc.scalar.copy(out=rows[b][:], in_=hold["rp", b][:].rearrange("p c n -> p (c n)"))
+            rr = psum.tile([128, C], F32, tag="s", name="rr", bufs=S_BANKS)
+            hold["rr", b] = rr
+            nc.tensor.matmul(out=rr[:], lhsT=sel_r[:], rhs=rows[b][:], start=True, stop=True)
+
+        def rstd_out(b):
+            nc.scalar.copy(out=rb[b][:], in_=hold["rr", b][:])
+
+        def embed_mm(q, h, t):
+            hp = psum.tile([128, GRP], F32, tag="h", name="hp", bufs=H_BANKS)
+            hold["hp", q, h, t] = hp
+            col = 512 * h + 128 * t
+            nc.tensor.matmul_mx(
+                out=hp[:],
+                lhsT=wq[:, col : col + 128].bitcast(FP8X4),
+                lhsT_scale=ws[:, col : col + 128],
+                rhs=mq[:, GRP * q : GRP * q + GRP].bitcast(FP8X4),
+                rhs_scale=ms[:, GRP * q : GRP * q + GRP],
+                start=True,
+                stop=True,
+            )
+
+        def embed_act(q, h, t):
+            if t == 0:
+                hold["ab", q, h] = work.tile([128, 4, GRP], BF16, tag="ab", name="ab", align_bytes=64, bufs=3)
+            k = 4 * h + t
+            nc.scalar.activation(
+                out=hold["ab", q, h][:, t, :], in_=hold["hp", q, h, t][:], func=ACT.Relu, scale=ag[:, k : k + 1], bias=gb[:, k : k + 1]
+            )
+
+        def a_inter(q, h):
+            at = work.tile([128, GRP, 4], BF16, tag="at", name="at", align_bytes=64, bufs=3)
+            hold["at", q, h] = at
+            interleave(("ai", q, h) in vector_list, at[:], hold["ab", q, h][:])
+
+        def a_quant(q, h):
+            if h == 0:
+                hold["aq", q] = work.tile([128, 2, GRP], U32, tag="aq", name="aq", align_bytes=64, bufs=3)
+                hold["sq", q] = work.tile([128, 2, GRP], U8, tag="sq", name="sq", align_bytes=64, bufs=3)
+            nc.vector.quantize_mx(
+                out=hold["aq", q][:, h, :].bitcast(FP8X4),
+                scales=hold["sq", q][:, h, :],
+                in_=hold["at", q, h][:].rearrange("p n t -> p (n t)"),
+            )
+
+        def stat_fill(q, cb):
+            bank = psum.tile([128, 4, 128], BF16, tag="s", name="xp", bufs=S_BANKS)
+            hold["xp", q, cb] = bank
+            for i in range(4):
+                nc.tensor.transpose(bank[:, i, :], xt[q][:, i, 128 * cb : 128 * cb + 128], idb[:])
+
+        def stat_drain(q, cb):
+            b, h = divmod(q, 2)
+            nc.vector.bn_stats(out=st[:, b, cb, h, :], in_=hold["xp", q, cb][:].rearrange("p i n -> p (i n)"))
+
+        def proj_fill(w, q, i):
+            bank = psum.tile([128, C], F32, tag="s", name="pb", bufs=S_BANKS)
+            hold["pb", w, q, i] = bank
+            aq, sq = hold["aq", q], hold["sq", q]
+            for h in range(2):
+                nc.tensor.matmul_mx(
+                    out=bank[:],
+                    lhsT=aq[:, h, 128 * i : 128 * i + 128].bitcast(FP8X4),
+                    lhsT_scale=sq[:, h, 128 * i : 128 * i + 128],
+                    rhs=vq[:, h, w, :].bitcast(FP8X4),
+                    rhs_scale=vs[:, h, w, :],
+                    start=(h == 0),
+                    stop=(h == 1),
+                )
+
+        def center_fill(q, i):
+            bank = psum.tile([128, C], F32, tag="s", name="cb", bufs=S_BANKS)
+            hold["cb", q, i] = bank
+            nc.tensor.matmul(out=bank[:], lhsT=idb[:], rhs=xt[q][:, i, :], start=True, stop=False)
+            nc.tensor.matmul(out=bank[:], lhsT=sel_m[:], rhs=rows[q // 2][:], start=False, stop=True)
+
+        def gamma_drain(q, i):
+            if i % 2 == 0:
+                hold["g2", q, i // 2] = work.tile([128, 2, C], F32, tag="g2", name="g2", bufs=2)
+            nc.vector.scalar_tensor_tensor(
+                out=hold["g2", q, i // 2][:, i % 2, :], in0=hold["pb", 0, q, i][:], scalar=1.0, in1=rb[q // 2][:], op0=ALU.add, op1=ALU.mult
+            )
+
+        def center_drain(q, i):
+            g2 = hold["g2", q, i // 2]
+            nc.vector.tensor_tensor(out=g2[:, i % 2, :], in0=hold["cb", q, i][:], in1=g2[:, i % 2, :], op=ALU.mult)
+
+        def beta_drain(q, i):
+            if i % 2 == 0:
+                hold["yy", q, i // 2] = work.tile([128, 2, C], F32, tag="yy", name="yy", bufs=3)
+            nc.vector.tensor_tensor(
+                out=hold["yy", q, i // 2][:, i % 2, :], in0=hold["pb", 1, q, i][:], in1=hold["g2", q, i // 2][:, i % 2, :], op=ALU.add
+            )
+
+        def leaky(q, pair):
+            b, hh = divmod(q, 2)
+            yy = hold["yy", q, pair]
+            oo = work.tile([128, 2, C], F32, tag="oo", name="oo", bufs=3)
+            if (q, pair) in LEAKY_ON_GPSIMD:
+                nc.gpsimd.tensor_scalar(out=oo[:], in0=yy[:], scalar1=0.0, scalar2=0.2, op0=ALU.is_ge, op1=ALU.max)
+                nc.gpsimd.tensor_tensor(out=oo[:], in0=yy[:], in1=oo[:], op=ALU.mult)
+            else:
+                nc.vector.scalar_tensor_tensor(out=oo[:], in0=yy[:], scalar=0.2, in1=yy[:], op0=ALU.mult, op1=ALU.max)
+            i0 = 4 * hh + 2 * pair
+            nc.sync.dma_start(out=out[b].rearrange("(p i) c -> p i c", i=TI)[:, i0 : i0 + 2, :], in_=oo[:])
+
+        steps = {
+            "mp": (m_product, 900), "mo": (m_out, 440), "mq": (m_quant, 470), "wi": (wm_inter, 1050), "wq": (wm_quant, 470),
+            "sg": (w_sign, 0), "vi": (w_inter, 1050), "vq": (w_quant, 470), "xa": (x_aggr, 450), "xr": (x_sqrt, 30), "xs": (x_split, 60),
+            "rt": (rows_turn, 0), "ro": (rows_out, 240), "rr": (rstd_out, 440), "ha": (embed_act, 450), "ai": (a_inter, 2000), "aq": (a_quant, 470),
+            "bn": (stat_drain, 450), "ga": (gamma_drain, 450), "ce": (center_drain, 450), "be": (beta_drain, 450), "lk": (leaky, 0),
+        }
+        fills = {
+            "ha": (embed_mm, "h", 220), "bn": (stat_fill, "s", 220), "ga": (lambda q, i: proj_fill(0, q, i), "s", 440),
+            "ce": (center_fill, "s", 430), "be": (lambda q, i: proj_fill(1, q, i), "s", 440),
+        }
+
+        def needs(s):
+            k, a = s[0], s[1:]
+            if k == "mo": return [("mp",) + a]
+            if k == "mq": return [("mo", a[0], 0), ("mo", a[0], 1)]
+            if k == "wq": return [("wi",) + a]
+            if k == "vi": return [("sg", a[0], a[1])]
+            if k == "vq": return [("vi",) + a]
+            if k == "aq": return [("ai",) + a]
+            if k == "ai": return [("ha", a[0], a[1], t) for t in range(4)]
+            if k == "xa": return [("bn", 2 * a[0] + h, c) for h in range(2) for c in range(4)]
+            if k == "xr": return [("xa",) + a]
+            if k == "xs": return [("xr",) + a]
+            if k == "rt": return [("xs",) + a]
+            if k == "ro": return [("rt",) + a]
+            if k == "rr": return [("ro",) + a]
+            if k == "ga": return [("rr", a[0] // 2)]
+            if k == "ce": return [("ga",) + a]
+            if k == "be": return [("ce",) + a]
+            if k == "lk": return [("be", a[0], 2 * a[1] + 1)]
+            return []
+
+        def fill_needs(s):
+            k, a = s[0], s[1:]
+            if k == "ha": return [("mq", a[0]), ("wq", a[1])]
+            if k == "ga": return [("aq", a[0], 0), ("aq", a[0], 1), ("vq", 0, 0), ("vq", 1, 0)]
+            if k == "be": return [("vq", 0, 1), ("vq", 1, 1)]
+            if k == "ce": return [("ro", a[0] // 2)]
+            if k == "bn": return BN_AFTER[a[0]]
+            return []
+
+        BN_AFTER = {0: [("mp", 1, 1)], 1: [("mp", 1, 1)], 2: [("be", 0, 3)], 3: [("be", 0, 3)]}
+        LATENCY = 200
+        E = lambda q, p: [("ga", q, 2 * p), ("ga", q, 2 * p + 1), ("ce", q, 2 * p), ("ce", q, 2 * p + 1), ("be", q, 2 * p), ("be", q, 2 * p + 1), ("lk", q, p)]
+        BN = lambda q: [("bn", q, c) for c in range(4)]
+        H = lambda q, h: [("ha", q, h, t) for t in range(4)]
+        vector_list = (
+            [("mp", 0, 0), ("mp", 0, 1), ("wi", 0), ("mq", 0), ("wq", 0), ("sg", 0, 0), ("sg", 1, 0), ("sg", 0, 1), ("sg", 1, 1)]
+            + [("wi", 1), ("mp", 1, 0), ("wq", 1), ("mp", 1, 1), ("vi", 0, 0), ("aq", 0, 0), ("vi", 1, 0), ("vq", 0, 0), ("vq", 1, 0)]
+            + BN(0) + [("mq", 1)] + BN(1) + [("xa", 0), ("aq", 0, 1), ("xs", 0), ("mp", 2, 0), ("mp", 2, 1), ("vq", 0, 1), ("vq", 1, 1)]
+            + E(0, 0) + [("mq", 2), ("aq", 1, 0)] + E(0, 1) + [("mp", 3, 0), ("aq", 1, 1), ("mp", 3, 1)] + BN(2) + E(1, 0) + [("mq", 3), ("aq", 2, 0)] + BN(3) + [("xa", 1), ("xs", 1)]
+            + E(1, 1) + [("aq", 2, 1)]
+            + E(2, 0) + [("aq", 3, 0)] + E(2, 1) + [("aq", 3, 1)] + E(3, 0) + E(3, 1)
+        )
+        scalar_list = (
+            [("mo", 0, 0), ("mo", 0, 1)] + H(0, 0) + [("ai", 0, 0), ("mo", 1, 0), ("mo", 1, 1)] + H(0, 1) + [("ai", 0, 1)]
+            + [("vi", 0, 1), ("xr", 0), ("vi", 1, 1), ("rt", 0), ("mo", 2, 0), ("ro", 0)] + H(1, 0)[:2] + [("rr", 0)] + H(1, 0)[2:] + [("ai", 1, 0), ("mo", 2, 1)] + H(1, 1) + [("ai", 1, 1)]
+            + [("mo", 3, 0)] + H(2, 0) + [("mo", 3, 1), ("ai", 2, 0)] + H(2, 1) + [("xr", 1), ("rt", 1), ("ai", 2, 1)] + [("ro", 1)] + H(3, 0) + [("rr", 1), ("ai", 3, 0)] + H(3, 1) + [("ai", 3, 1)]
+        )
+        rings = {"h": [s for s in scalar_list if s[0] == "ha"], "s": [s for s in vector_list if s[0] in ("bn", "ga", "ce", "be")]}
+        room = {"h": [0] * H_BANKS, "s": [0] * S_BANKS}
+        lists = {"v": list(vector_list), "a": list(scalar_list)}
+        clock = {"v": 3000, "a": 3000, "pe": 3000}
+        done = {}
+        filled = {}
+        spare = [T_BANKS]
+        takes = {"mp": 1}
+        gives = {"mo": 1}
+
+        def when(need):
+            if all(n in done for n in need):
+                return max([done[n] for n in need] + [0])
+            return None
+
+        def start_of(n):
+            if n in rings:
+                if not rings[n] or not room[n]:
+                    return None
+                t = when(fill_needs(rings[n][0]))
+                return None if t is None else max(t, room[n][0], clock["pe"])
+            if not lists[n]:
+                return None
+            s = lists[n][0]
+            t = when(needs(s))
+            if t is None or (s[0] in fills and s not in filled) or takes.get(s[0], 0) > spare[0] or (s[0] == "rt" and not room["s"]):
+                return None
+            return max(t, clock[n], filled.get(s, 0))
+
+        with tc.manual_schedule():
+            while lists["v"] or lists["a"]:
+                starts = [(start_of(n), i, n) for i, n in enumerate(("h", "s", "a", "v")) if start_of(n) is not None]
+                assert starts, (lists["v"][:1], lists["a"][:1])
+                t, i, n = min(starts)
+                if n in rings:
+                    s = rings[n].pop(0)
+                    room[n].pop(0)
+                    fills[s[0]][0](*s[1:])
+                    clock["pe"] = t + fills[s[0]][2]
+                    filled[s] = clock["pe"] + LATENCY
+                else:
+                    s = lists[n].pop(0)
+                    steps[s[0]][0](*s[1:])
+                    spare[0] += gives.get(s[0], 0) - takes.get(s[0], 0)
+                    clock[n] = t + steps[s[0]][1]
+                    done[s] = clock[n] + LATENCY
+                    if s[0] == "mp":
+                        clock["pe"] = max(clock["pe"] + 440, done[s] + 220)
+                        done[s] = clock["pe"] + LATENCY
+                    if s[0] == "rt":
+                        room["s"].pop(0)
+                    if s[0] == "rr":
+                        room["s"].append(done[s])
+                    if s[0] in fills:
+                        room[fills[s[0]][1]].append(done[s])

@@ -22,8 +22,8 @@ S_BANKS = 4
 GRP = 512
 A_ON_VECTOR = ()
 W_ON_SCALAR = ((0, 1), (1, 1))
-LEAKY_ON_GPSIMD = ((0, 0), (0, 1), (1, 0), (1, 1), (2, 0), (2, 1))
-SIGN_ON_GPSIMD = True
+LEAKY_ON_GPSIMD = ()
+SIGN_ON_GPSIMD = False
 
 
 def tile_spademodulationpointwise_kernel(tc, x, m_bytes, m_scale, wm, bm, g, wg, wb, out):
@@ -115,7 +115,8 @@ def tile_spademodulationpointwise_kernel(tc, x, m_bytes, m_scale, wm, bm, g, wg,
                 nc.scalar.copy(out=o, in_=s)
 
         def m_product(q, pair):
-            bank = psum.tile([128, 2, 2, 128], F32, tag="t", name="mt", bufs=T_BANKS)
+            tag = "s" if q < 2 else "t"
+            bank = psum.tile([128, 2, 2, 128], F32, tag=tag, name="mt", bufs=S_BANKS if q < 2 else T_BANKS)
             hold["t", q, pair] = bank
             for il in range(2):
                 mp = work.tile([128, S], BF16, tag="mp", name="mp", align_bytes=64, bufs=4)
@@ -307,9 +308,9 @@ def tile_spademodulationpointwise_kernel(tc, x, m_bytes, m_scale, wm, bm, g, wg,
 
         steps = {
             "mp": (m_product, 900), "mo": (m_out, 440), "mq": (m_quant, 470), "wi": (wm_inter, 1050), "wq": (wm_quant, 470),
-            "sg": (w_sign, 0), "vi": (w_inter, 1050), "vq": (w_quant, 470), "xa": (x_aggr, 450), "xr": (x_sqrt, 30), "xs": (x_split, 60),
+            "sg": (w_sign, 500), "vi": (w_inter, 1050), "vq": (w_quant, 470), "xa": (x_aggr, 450), "xr": (x_sqrt, 30), "xs": (x_split, 60),
             "rt": (rows_turn, 0), "ro": (rows_out, 240), "rr": (rstd_out, 440), "ha": (embed_act, 450), "ai": (a_inter, 2000), "aq": (a_quant, 470),
-            "bn": (stat_drain, 450), "ga": (gamma_drain, 450), "ce": (center_drain, 450), "be": (beta_drain, 450), "lk": (leaky, 0),
+            "bn": (stat_drain, 450), "ga": (gamma_drain, 450), "ce": (center_drain, 450), "be": (beta_drain, 450), "lk": (leaky, 870),
         }
         fills = {
             "ha": (embed_mm, "h", 220), "bn": (stat_fill, "s", 220), "ga": (lambda q, i: proj_fill(0, q, i), "s", 440),
@@ -346,23 +347,23 @@ def tile_spademodulationpointwise_kernel(tc, x, m_bytes, m_scale, wm, bm, g, wg,
             if k == "bn": return BN_AFTER[a[0]]
             return []
 
-        BN_AFTER = {0: [("mp", 1, 1)], 1: [("mp", 1, 1)], 2: [("be", 0, 3)], 3: [("be", 0, 3)]}
+        BN_AFTER = {0: [("mp", 1, 1)], 1: [("mp", 1, 1)], 2: [("mp", 2, 0)], 3: [("mp", 2, 1)]}
         LATENCY = 200
         E = lambda q, p: [("ga", q, 2 * p), ("ga", q, 2 * p + 1), ("ce", q, 2 * p), ("ce", q, 2 * p + 1), ("be", q, 2 * p), ("be", q, 2 * p + 1), ("lk", q, p)]
         BN = lambda q: [("bn", q, c) for c in range(4)]
         H = lambda q, h: [("ha", q, h, t) for t in range(4)]
         vector_list = (
-            [("mp", 0, 0), ("mp", 0, 1), ("wi", 0), ("mq", 0), ("wq", 0), ("sg", 0, 0), ("sg", 1, 0), ("sg", 0, 1), ("sg", 1, 1)]
-            + [("wi", 1), ("mp", 1, 0), ("wq", 1), ("mp", 1, 1), ("vi", 0, 0), ("aq", 0, 0), ("vi", 1, 0), ("vq", 0, 0), ("vq", 1, 0)]
-            + BN(0) + [("mq", 1)] + BN(1) + [("xa", 0), ("aq", 0, 1), ("xs", 0), ("mp", 2, 0), ("mp", 2, 1), ("vq", 0, 1), ("vq", 1, 1)]
-            + E(0, 0) + [("mq", 2), ("aq", 1, 0)] + E(0, 1) + [("mp", 3, 0), ("aq", 1, 1), ("mp", 3, 1)] + BN(2) + E(1, 0) + [("mq", 3), ("aq", 2, 0)] + BN(3) + [("xa", 1), ("xs", 1)]
-            + E(1, 1) + [("aq", 2, 1)]
-            + E(2, 0) + [("aq", 3, 0)] + E(2, 1) + [("aq", 3, 1)] + E(3, 0) + E(3, 1)
+            [("mp", 0, 0), ("mp", 0, 1), ("wi", 0), ("mq", 0), ("wq", 0), ("wi", 1), ("mp", 1, 0), ("wq", 1), ("mp", 1, 1)]
+            + [("sg", 0, 0), ("sg", 1, 0), ("sg", 0, 1), ("sg", 1, 1)] + BN(0) + [("aq", 0, 0)] + BN(1) + [("mq", 1), ("xa", 0), ("mp", 2, 0)]
+            + BN(2) + [("aq", 0, 1), ("xs", 0), ("vq", 0, 0), ("mp", 2, 1)] + BN(3) + [("vq", 1, 0), ("xa", 1), ("mq", 2), ("mp", 3, 0), ("vq", 0, 1), ("xs", 1), ("mp", 3, 1), ("vq", 1, 1)]
+            + E(0, 0) + [("aq", 1, 0)] + E(0, 1) + [("aq", 1, 1)] + E(1, 0) + [("mq", 3), ("aq", 2, 0)]
+            + E(1, 1) + [("aq", 2, 1)] + E(2, 0) + [("aq", 3, 0)] + E(2, 1) + [("aq", 3, 1)] + E(3, 0) + E(3, 1)
         )
         scalar_list = (
             [("mo", 0, 0), ("mo", 0, 1)] + H(0, 0) + [("ai", 0, 0), ("mo", 1, 0), ("mo", 1, 1)] + H(0, 1) + [("ai", 0, 1)]
-            + [("vi", 0, 1), ("xr", 0), ("vi", 1, 1), ("rt", 0), ("mo", 2, 0), ("ro", 0)] + H(1, 0)[:2] + [("rr", 0)] + H(1, 0)[2:] + [("ai", 1, 0), ("mo", 2, 1)] + H(1, 1) + [("ai", 1, 1)]
-            + [("mo", 3, 0)] + H(2, 0) + [("mo", 3, 1), ("ai", 2, 0)] + H(2, 1) + [("xr", 1), ("rt", 1), ("ai", 2, 1)] + [("ro", 1)] + H(3, 0) + [("rr", 1), ("ai", 3, 0)] + H(3, 1) + [("ai", 3, 1)]
+            + [("vi", 0, 0), ("xr", 0), ("mo", 2, 0), ("vi", 1, 0), ("rt", 0), ("mo", 2, 1), ("ro", 0), ("vi", 0, 1), ("rr", 0), ("xr", 1), ("vi", 1, 1), ("mo", 3, 0), ("rt", 1)] + H(1, 0)[:2] + [("ro", 1)] + H(1, 0)[2:]
+            + [("rr", 1), ("ai", 1, 0)] + H(1, 1) + [("mo", 3, 1), ("ai", 1, 1)]
+            + H(2, 0) + [("ai", 2, 0)] + H(2, 1) + [("ai", 2, 1)] + H(3, 0) + [("ai", 3, 0)] + H(3, 1) + [("ai", 3, 1)]
         )
         rings = {"h": [s for s in scalar_list if s[0] == "ha"], "s": [s for s in vector_list if s[0] in ("bn", "ga", "ce", "be")]}
         room = {"h": [0] * H_BANKS, "s": [0] * S_BANKS}
@@ -371,8 +372,6 @@ def tile_spademodulationpointwise_kernel(tc, x, m_bytes, m_scale, wm, bm, g, wg,
         done = {}
         filled = {}
         spare = [T_BANKS]
-        takes = {"mp": 1}
-        gives = {"mo": 1}
 
         def when(need):
             if all(n in done for n in need):
@@ -389,7 +388,7 @@ def tile_spademodulationpointwise_kernel(tc, x, m_bytes, m_scale, wm, bm, g, wg,
                 return None
             s = lists[n][0]
             t = when(needs(s))
-            if t is None or (s[0] in fills and s not in filled) or takes.get(s[0], 0) > spare[0] or (s[0] == "rt" and not room["s"]):
+            if t is None or (s[0] in fills and s not in filled) or (s[0] == "mp" and s[1] >= 2 and not spare[0]) or ((s[0] == "rt" or (s[0] == "mp" and s[1] < 2)) and not room["s"]):
                 return None
             return max(t, clock[n], filled.get(s, 0))
 
@@ -407,7 +406,12 @@ def tile_spademodulationpointwise_kernel(tc, x, m_bytes, m_scale, wm, bm, g, wg,
                 else:
                     s = lists[n].pop(0)
                     steps[s[0]][0](*s[1:])
-                    spare[0] += gives.get(s[0], 0) - takes.get(s[0], 0)
+                    if s[0] == "mp" and s[1] < 2:
+                        room["s"].pop(0)
+                    elif s[0] == "mp":
+                        spare[0] -= 1
+                    elif s[0] == "mo" and s[1] >= 2:
+                        spare[0] += 1
                     clock[n] = t + steps[s[0]][1]
                     done[s] = clock[n] + LATENCY
                     if s[0] == "mp":
@@ -415,7 +419,7 @@ def tile_spademodulationpointwise_kernel(tc, x, m_bytes, m_scale, wm, bm, g, wg,
                         done[s] = clock["pe"] + LATENCY
                     if s[0] == "rt":
                         room["s"].pop(0)
-                    if s[0] == "rr":
+                    if s[0] == "rr" or (s[0] == "mo" and s[1] < 2):
                         room["s"].append(done[s])
                     if s[0] in fills:
                         room[fills[s[0]][1]].append(done[s])

from contextlib import ExitStack

import concourse.mybir as mybir
from concourse.masks import make_identity

B, P, S, K, C = 2, 1024, 512, 1024, 512
FLOPS = 2 * B * P * S * K + 2 * 2 * B * P * K * C

F32 = mybir.dt.float32
BF16 = mybir.dt.bfloat16
U32 = mybir.dt.uint32
U8 = mybir.dt.uint8
FP8 = mybir.dt.float8_e4m3fn
FP8X4 = mybir.dt.float8_e4m3fn_x4
ACT = mybir.ActivationFunctionType
ALU = mybir.AluOpType

TI = 8
T_BANKS = 1
H_BANKS = 3
S_BANKS = 4
GRP = 512
A_ON_VECTOR = ()
W_ON_SCALAR = ((0, 1), (1, 1))
LEAKY_ON_GPSIMD = ()
SIGN_ON_GPSIMD = False


def tile_spademodulationpointwise_kernel(tc, x, m_bytes, m_scale, wm, bm, g, wg, wb, out):
    nc = tc.nc
    with ExitStack() as ctx:
        keep = ctx.enter_context(tc.tile_pool(name="keep", bufs=1))
        work = ctx.enter_context(tc.tile_pool(name="work", bufs=3))
        psum = ctx.enter_context(tc.psum_pool(name="psum", bufs=2))

        sc = keep.tile([128, S], F32, name="sc")
        nc.scalar.dma_start(out=sc[:], in_=m_scale.rearrange("o q k -> (o q k)").partition_broadcast(128))
        gv = keep.tile([128, 8], BF16, name="gv")
        bv = keep.tile([128, 8], BF16, name="bv")
        nc.scalar.dma_start(out=gv[:].rearrange("p (h t) -> p h t", t=4), in_=g.rearrange("(h p t) -> p h t", p=128, t=4))
        nc.scalar.dma_start(out=bv[:].rearrange("p (h t) -> p h t", t=4), in_=bm.rearrange("(h p t) -> p h t", p=128, t=4))

        mb = [keep.tile([128, 4, S], U8, name=f"mb{q}", align_bytes=64) for q in range(4)]
        wr = [keep.tile([128, 4, 512], BF16, name=f"wr{h}", align_bytes=64) for h in range(2)]
        xt = [keep.tile([128, 4, C], BF16, name=f"xt{q}", align_bytes=64) for q in range(4)]
        vr = [keep.tile([128, 2, 4, C], BF16, name=f"vr{h}", align_bytes=64) for h in range(2)]
        wm_v = wm.rearrange("(p j) n -> p j n", j=4)

        def load_m(q):
            b, h = divmod(q, 2)
            nc.sync.dma_start(out=mb[q][:], in_=m_bytes[b].rearrange("(p i) k -> p i k", i=TI)[:, 4 * h : 4 * h + 4, :])

        def load_x(q):
            b, h = divmod(q, 2)
            nc.sync.dma_start(out=xt[q][:], in_=x[b].rearrange("(p i) c -> p i c", i=TI)[:, 4 * h : 4 * h + 4, :])

        load_m(0)
        nc.sync.dma_start(out=wr[0][:], in_=wm_v[:, :, 0:512])
        nc.sync.dma_start(out=wr[1][:], in_=wm_v[:, :, 512:1024])
        load_m(1)
        for w, src in enumerate((wg, wb)):
            for h in range(2):
                nc.sync.dma_start(out=vr[h][:, w], in_=src[512 * h : 512 * h + 512, :].rearrange("(p j) c -> p j c", j=4))
        load_x(0)
        load_x(1)
        load_m(2)
        load_m(3)
        load_x(2)
        load_x(3)

        hold = {}

        idf = keep.tile([128, 128], F32, name="idf")
        make_identity(nc, idf[:])
        idb = keep.tile([128, 128], BF16, name="idb")
        make_identity(nc, idb[:])
        sel_r = keep.tile([128, 128], BF16, name="sel_r")
        sel_m = keep.tile([128, 128], BF16, name="sel_m")
        nc.gpsimd.memset(sel_r[:], 0.0)
        nc.gpsimd.memset(sel_r[0:3, :], 1.0)
        nc.gpsimd.memset(sel_m[:], 0.0)
        nc.gpsimd.memset(sel_m[32:35, :], 1.0)
        rs = [keep.tile([128, 4, 128], BF16, name=f"rs{b}") for b in range(2)]
        for b in range(2):
            nc.gpsimd.memset(rs[b][:], 0.0)

        ng = keep.tile([128, 8], F32, name="ng")
        ag = keep.tile([128, 8], F32, name="ag")
        gb = keep.tile([128, 8], F32, name="gb")
        sg0 = keep.tile([128, 8], F32, name="sg0")
        sg = keep.tile([128, 8], F32, name="sg")
        nc.vector.tensor_scalar(out=ng[:], in0=gv[:], scalar1=-1.0, scalar2=None, op0=ALU.mult)
        nc.vector.tensor_scalar(out=sg0[:], in0=gv[:], scalar1=0.0, scalar2=2.0, op0=ALU.is_ge, op1=ALU.mult)
        nc.vector.tensor_tensor(out=ag[:], in0=gv[:], in1=ng[:], op=ALU.max)
        nc.vector.tensor_scalar(out=sg[:], in0=sg0[:], scalar1=-1.0, scalar2=None, op0=ALU.add)
        nc.vector.tensor_tensor(out=gb[:], in0=ag[:], in1=bv[:], op=ALU.mult)

        mq = keep.tile([128, 2048], U32, name="mq", align_bytes=64)
        ms = keep.tile([128, 2048], U8, name="ms", align_bytes=64)
        wq = keep.tile([128, 1024], U32, name="wq", align_bytes=64)
        ws = keep.tile([128, 1024], U8, name="ws", align_bytes=64)
        vq = keep.tile([128, 2, 2, 512], U32, name="vq", align_bytes=64)
        vs = keep.tile([128, 2, 2, 512], U8, name="vs", align_bytes=64)
        st = keep.tile([128, 2, 4, 2, 6], F32, name="st")
        mv = keep.tile([128, 2, 4, 2], F32, name="mv")
        rb = [keep.tile([128, C], F32, name=f"rb{b}") for b in range(2)]
        rows = [keep.tile([128, C], BF16, name=f"rows{b}") for b in range(2)]

        def interleave(on_vector, dst, src):
            o = dst.rearrange("p (c i) t -> p c t i", i=4)
            s = src.rearrange("p t (c i) -> p c t i", i=4)
            if on_vector:
                nc.vector.tensor_copy(out=o, in_=s)
            else:
                nc.scalar.copy(out=o, in_=s)

        def m_product(q, pair):
            tag = "s" if q < 2 else "t"
            bank = psum.tile([128, 2, 2, 128], F32, tag=tag, name="mt", bufs=S_BANKS if q < 2 else T_BANKS)
            hold["t", q, pair] = bank
            for il in range(2):
                mp = work.tile([128, S], BF16, tag="mp", name="mp", align_bytes=64, bufs=4)
                nc.vector.tensor_tensor(out=mp[:], in0=mb[q][:, 2 * pair + il, :].bitcast(FP8), in1=sc[:], op=ALU.mult)
                w = mp[:].bitcast(F32)
                for u in range(2):
                    nc.tensor.transpose(bank[:, il, u, :], w[:, u : 256 : 2], idf[:])

        def m_out(q, pair):
            if pair == 0:
                hold["mg", q] = work.tile([128, GRP, 4], BF16, tag="mg", name="mg", align_bytes=64, bufs=2)
            mgw = hold["mg", q][:].rearrange("p n t -> p (n t)").bitcast(F32)
            nc.scalar.copy(
                out=mgw[:, 512 * pair : 512 * pair + 512].rearrange("p (i r u) -> p i r u", i=2, u=2),
                in_=hold["t", q, pair][:].rearrange("p i u r -> p i r u"),
            )

        def m_quant(q):
            nc.vector.quantize_mx(
                out=mq[:, GRP * q : GRP * q + GRP].bitcast(FP8X4),
                scales=ms[:, GRP * q : GRP * q + GRP],
                in_=hold["mg", q][:].rearrange("p n t -> p (n t)"),
            )

        def wm_inter(h):
            wgr = work.tile([128, 4, 128, 4], BF16, tag="wgr", name="wgr", align_bytes=64, bufs=2)
            hold["wgr", h] = wgr
            nc.vector.tensor_copy(out=wgr[:], in_=wr[h][:].rearrange("p j (m t) -> p t m j", t=4))

        def wm_quant(h):
            nc.vector.quantize_mx(
                out=wq[:, 512 * h : 512 * h + 512].bitcast(FP8X4),
                scales=ws[:, 512 * h : 512 * h + 512],
                in_=hold["wgr", h][:].rearrange("p t m j -> p (t m j)"),
            )

        def w_sign(h, w):
            for j in range(4):
                k = 4 * h + j
                if SIGN_ON_GPSIMD:
                    nc.gpsimd.tensor_scalar(out=vr[h][:, w, j, :], in0=vr[h][:, w, j, :], scalar1=sg[:, k : k + 1], scalar2=0.0, op0=ALU.mult, op1=ALU.add)
                else:
                    nc.vector.tensor_scalar(out=vr[h][:, w, j, :], in0=vr[h][:, w, j, :], scalar1=sg[:, k : k + 1], scalar2=None, op0=ALU.mult)

        def w_inter(h, w):
            vg = work.tile([128, C, 4], BF16, tag="vg", name="vg", align_bytes=64, bufs=3)
            hold["vg", h, w] = vg
            interleave(("vi", h, w) in vector_list, vg[:], vr[h][:, w])

        def w_quant(h, w):
            nc.vector.quantize_mx(
                out=vq[:, h, w, :].bitcast(FP8X4), scales=vs[:, h, w, :], in_=hold["vg", h, w][:].rearrange("p c t -> p (c t)")
            )

        def x_aggr(b):
            for cb in range(4):
                nc.vector.bn_aggr(out=mv[:, b, cb, :], in_=st[:, b, cb].rearrange("p h s -> p (h s)"))
            for name in ("ve", "sd"):
                hold[name, b] = keep.tile([128, 4], F32, name=f"{name}{b}")
            for name in ("rm", "r1", "r2"):
                hold[name, b] = keep.tile([128, 4, 2], F32, name=f"{name}{b}")
            nc.vector.tensor_scalar(out=hold["ve", b][:], in0=mv[:, b, :, 1], scalar1=1e-5, scalar2=None, op0=ALU.add)
            nc.vector.tensor_scalar(out=hold["rm", b][:, :, 1], in0=mv[:, b, :, 0], scalar1=-1.0, scalar2=None, op0=ALU.mult)

        def x_sqrt(b):
            nc.scalar.activation(out=hold["sd", b][:], in_=hold["ve", b][:], func=ACT.Sqrt)

        def x_split(b):
            rm, r1, r2 = hold["rm", b], hold["r1", b], hold["r2", b]
            nc.vector.reciprocal(out=rm[:, :, 0], in_=hold["sd", b][:])
            nc.gpsimd.tensor_copy(out=rs[b][:, :, 0:64:32], in_=rm[:])
            nc.gpsimd.tensor_tensor(out=r1[:], in0=rm[:], in1=rs[b][:, :, 0:64:32], op=ALU.subtract)
            nc.gpsimd.tensor_copy(out=rs[b][:, :, 1:64:32], in_=r1[:])
            nc.gpsimd.tensor_tensor(out=r2[:], in0=r1[:], in1=rs[b][:, :, 1:64:32], op=ALU.subtract)
            nc.gpsimd.tensor_copy(out=rs[b][:, :, 2:64:32], in_=r2[:])

        def rows_turn(b):
            rp = psum.tile([128, 4, 128], BF16, tag="s", name="rp", bufs=S_BANKS)
            hold["rp", b] = rp
            for cb in range(4):
                nc.tensor.transpose(rp[:, cb, :], rs[b][:, cb, :], idb[:])

        def rows_out(b):
            nc.scalar.copy(out=rows[b][:], in_=hold["rp", b][:].rearrange("p c n -> p (c n)"))
            rr = psum.tile([128, C], F32, tag="s", name="rr", bufs=S_BANKS)
            hold["rr", b] = rr
            nc.tensor.matmul(out=rr[:], lhsT=sel_r[:], rhs=rows[b][:], start=True, stop=True)

        def rstd_out(b):
            nc.scalar.copy(out=rb[b][:], in_=hold["rr", b][:])

        def embed_mm(q, h, t):
            hp = psum.tile([128, GRP], F32, tag="h", name="hp", bufs=H_BANKS)
            hold["hp", q, h, t] = hp
            col = 512 * h + 128 * t
            nc.tensor.matmul_mx(
                out=hp[:],
                lhsT=wq[:, col : col + 128].bitcast(FP8X4),
                lhsT_scale=ws[:, col : col + 128],
                rhs=mq[:, GRP * q : GRP * q + GRP].bitcast(FP8X4),
                rhs_scale=ms[:, GRP * q : GRP * q + GRP],
                start=True,
                stop=True,
            )

        def embed_act(q, h, t):
            if t == 0:
                hold["ab", q, h] = work.tile([128, 4, GRP], BF16, tag="ab", name="ab", align_bytes=64, bufs=3)
            k = 4 * h + t
            nc.scalar.activation(
                out=hold["ab", q, h][:, t, :], in_=hold["hp", q, h, t][:], func=ACT.Relu, scale=ag[:, k : k + 1], bias=gb[:, k : k + 1]
            )

        def a_inter(q, h):
            at = work.tile([128, GRP, 4], BF16, tag="at", name="at", align_bytes=64, bufs=3)
            hold["at", q, h] = at
            interleave(("ai", q, h) in vector_list, at[:], hold["ab", q, h][:])

        def a_quant(q, h):
            if h == 0:
                hold["aq", q] = work.tile([128, 2, GRP], U32, tag="aq", name="aq", align_bytes=64, bufs=3)
                hold["sq", q] = work.tile([128, 2, GRP], U8, tag="sq", name="sq", align_bytes=64, bufs=3)
            nc.vector.quantize_mx(
                out=hold["aq", q][:, h, :].bitcast(FP8X4),
                scales=hold["sq", q][:, h, :],
                in_=hold["at", q, h][:].rearrange("p n t -> p (n t)"),
            )

        def stat_fill(q, cb):
            bank = psum.tile([128, 4, 128], BF16, tag="s", name="xp", bufs=S_BANKS)
            hold["xp", q, cb] = bank
            for i in range(4):
                nc.tensor.transpose(bank[:, i, :], xt[q][:, i, 128 * cb : 128 * cb + 128], idb[:])

        def stat_drain(q, cb):
            b, h = divmod(q, 2)
            nc.vector.bn_stats(out=st[:, b, cb, h, :], in_=hold["xp", q, cb][:].rearrange("p i n -> p (i n)"))

        def proj_fill(w, q, i):
            bank = psum.tile([128, C], F32, tag="s", name="pb", bufs=S_BANKS)
            hold["pb", w, q, i] = bank
            aq, sq = hold["aq", q], hold["sq", q]
            for h in range(2):
                nc.tensor.matmul_mx(
                    out=bank[:],
                    lhsT=aq[:, h, 128 * i : 128 * i + 128].bitcast(FP8X4),
                    lhsT_scale=sq[:, h, 128 * i : 128 * i + 128],
                    rhs=vq[:, h, w, :].bitcast(FP8X4),
                    rhs_scale=vs[:, h, w, :],
                    start=(h == 0),
                    stop=(h == 1),
                )

        def center_fill(q, i):
            bank = psum.tile([128, C], F32, tag="s", name="cb", bufs=S_BANKS)
            hold["cb", q, i] = bank
            nc.tensor.matmul(out=bank[:], lhsT=idb[:], rhs=xt[q][:, i, :], start=True, stop=False)
            nc.tensor.matmul(out=bank[:], lhsT=sel_m[:], rhs=rows[q // 2][:], start=False, stop=True)

        def gamma_drain(q, i):
            if i % 2 == 0:
                hold["g2", q, i // 2] = work.tile([128, 2, C], F32, tag="g2", name="g2", bufs=2)
            nc.vector.scalar_tensor_tensor(
                out=hold["g2", q, i // 2][:, i % 2, :], in0=hold["pb", 0, q, i][:], scalar=1.0, in1=rb[q // 2][:], op0=ALU.add, op1=ALU.mult
            )

        def center_drain(q, i):
            g2 = hold["g2", q, i // 2]
            nc.vector.tensor_tensor(out=g2[:, i % 2, :], in0=hold["cb", q, i][:], in1=g2[:, i % 2, :], op=ALU.mult)

        def beta_drain(q, i):
            if i % 2 == 0:
                hold["yy", q, i // 2] = work.tile([128, 2, C], F32, tag="yy", name="yy", bufs=3)
            nc.vector.tensor_tensor(
                out=hold["yy", q, i // 2][:, i % 2, :], in0=hold["pb", 1, q, i][:], in1=hold["g2", q, i // 2][:, i % 2, :], op=ALU.add
            )

        def leaky(q, pair):
            b, hh = divmod(q, 2)
            yy = hold["yy", q, pair]
            oo = work.tile([128, 2, C], F32, tag="oo", name="oo", bufs=3)
            if (q, pair) in LEAKY_ON_GPSIMD:
                nc.gpsimd.tensor_scalar(out=oo[:], in0=yy[:], scalar1=0.0, scalar2=0.2, op0=ALU.is_ge, op1=ALU.max)
                nc.gpsimd.tensor_tensor(out=oo[:], in0=yy[:], in1=oo[:], op=ALU.mult)
            else:
                nc.vector.scalar_tensor_tensor(out=oo[:], in0=yy[:], scalar=0.2, in1=yy[:], op0=ALU.mult, op1=ALU.max)
            i0 = 4 * hh + 2 * pair
            nc.sync.dma_start(out=out[b].rearrange("(p i) c -> p i c", i=TI)[:, i0 : i0 + 2, :], in_=oo[:])

        steps = {
            "mp": (m_product, 900), "mo": (m_out, 440), "mq": (m_quant, 470), "wi": (wm_inter, 1050), "wq": (wm_quant, 470),
            "sg": (w_sign, 500), "vi": (w_inter, 1050), "vq": (w_quant, 470), "xa": (x_aggr, 450), "xr": (x_sqrt, 30), "xs": (x_split, 60),
            "rt": (rows_turn, 0), "ro": (rows_out, 240), "rr": (rstd_out, 440), "ha": (embed_act, 450), "ai": (a_inter, 2000), "aq": (a_quant, 470),
            "bn": (stat_drain, 450), "ga": (gamma_drain, 450), "ce": (center_drain, 450), "be": (beta_drain, 450), "lk": (leaky, 870),
        }
        fills = {
            "ha": (embed_mm, "h", 220), "bn": (stat_fill, "s", 220), "ga": (lambda q, i: proj_fill(0, q, i), "s", 440),
            "ce": (center_fill, "s", 430), "be": (lambda q, i: proj_fill(1, q, i), "s", 440),
        }

        def needs(s):
            k, a = s[0], s[1:]
            if k == "mo": return [("mp",) + a]
            if k == "mq": return [("mo", a[0], 0), ("mo", a[0], 1)]
            if k == "wq": return [("wi",) + a]
            if k == "vi": return [("sg", a[0], a[1])]
            if k == "vq": return [("vi",) + a]
            if k == "aq": return [("ai",) + a]
            if k == "ai": return [("ha", a[0], a[1], t) for t in range(4)]
            if k == "xa": return [("bn", 2 * a[0] + h, c) for h in range(2) for c in range(4)]
            if k == "xr": return [("xa",) + a]
            if k == "xs": return [("xr",) + a]
            if k == "rt": return [("xs",) + a]
            if k == "ro": return [("rt",) + a]
            if k == "rr": return [("ro",) + a]
            if k == "ga": return [("rr", a[0] // 2)]
            if k == "ce": return [("ga",) + a]
            if k == "be": return [("ce",) + a]
            if k == "lk": return [("be", a[0], 2 * a[1] + 1)]
            return []

        def fill_needs(s):
            k, a = s[0], s[1:]
            if k == "ha": return [("mq", a[0]), ("wq", a[1])]
            if k == "ga": return [("aq", a[0], 0), ("aq", a[0], 1), ("vq", 0, 0), ("vq", 1, 0)]
            if k == "be": return [("vq", 0, 1), ("vq", 1, 1)]
            if k == "ce": return [("ro", a[0] // 2)]
            if k == "bn": return BN_AFTER[a[0]]
            return []

        BN_AFTER = {0: [("mp", 1, 1)], 1: [("mp", 1, 1)], 2: [("mp", 2, 0)], 3: [("mp", 2, 1)]}
        LATENCY = 200
        E = lambda q, p: [("ga", q, 2 * p), ("ga", q, 2 * p + 1), ("ce", q, 2 * p), ("ce", q, 2 * p + 1), ("be", q, 2 * p), ("be", q, 2 * p + 1), ("lk", q, p)]
        BN = lambda q: [("bn", q, c) for c in range(4)]
        H = lambda q, h: [("ha", q, h, t) for t in range(4)]
        vector_list = (
            [("mp", 0, 0), ("mp", 0, 1), ("wi", 0), ("mq", 0), ("wq", 0), ("wi", 1), ("mp", 1, 0), ("wq", 1), ("mp", 1, 1)]
            + [("sg", 0, 0), ("sg", 1, 0), ("sg", 0, 1), ("sg", 1, 1)] + BN(0) + [("aq", 0, 0)] + BN(1) + [("mq", 1), ("xa", 0), ("mp", 2, 0)]
            + BN(2) + [("aq", 0, 1), ("xs", 0), ("vq", 0, 0), ("mp", 2, 1)] + BN(3) + [("vq", 1, 0), ("xa", 1), ("mq", 2), ("mp", 3, 0), ("vq", 0, 1), ("xs", 1), ("mp", 3, 1), ("vq", 1, 1)]
            + E(0, 0) + [("aq", 1, 0)] + E(0, 1) + [("aq", 1, 1)] + E(1, 0) + [("mq", 3), ("aq", 2, 0)]
            + E(1, 1) + [("aq", 2, 1)] + E(2, 0) + [("aq", 3, 0)] + E(2, 1) + [("aq", 3, 1)] + E(3, 0) + E(3, 1)
        )
        scalar_list = (
            [("mo", 0, 0), ("mo", 0, 1)] + H(0, 0) + [("ai", 0, 0), ("mo", 1, 0), ("mo", 1, 1)] + H(0, 1) + [("ai", 0, 1)]
            + [("vi", 0, 0), ("xr", 0), ("mo", 2, 0), ("vi", 1, 0), ("rt", 0), ("mo", 2, 1), ("ro", 0), ("vi", 0, 1), ("rr", 0), ("xr", 1), ("vi", 1, 1), ("mo", 3, 0), ("rt", 1)] + H(1, 0)[:2] + [("ro", 1)] + H(1, 0)[2:]
            + [("rr", 1), ("ai", 1, 0)] + H(1, 1) + [("mo", 3, 1), ("ai", 1, 1)]
            + H(2, 0) + [("ai", 2, 0)] + H(2, 1) + [("ai", 2, 1)] + H(3, 0) + [("ai", 3, 0)] + H(3, 1) + [("ai", 3, 1)]
        )
        rings = {"h": [s for s in scalar_list if s[0] == "ha"], "s": [s for s in vector_list if s[0] in ("bn", "ga", "ce", "be")]}
        room = {"h": [0] * H_BANKS, "s": [0] * S_BANKS}
        lists = {"v": list(vector_list), "a": list(scalar_list)}
        clock = {"v": 3000, "a": 3000, "pe": 3000}
        done = {}
        filled = {}
        spare = [T_BANKS]

        def when(need):
            if all(n in done for n in need):
                return max([done[n] for n in need] + [0])
            return None

        def start_of(n):
            if n in rings:
                if not rings[n] or not room[n]:
                    return None
                t = when(fill_needs(rings[n][0]))
                return None if t is None else max(t, room[n][0], clock["pe"])
            if not lists[n]:
                return None
            s = lists[n][0]
            t = when(needs(s))
            if t is None or (s[0] in fills and s not in filled) or (s[0] == "mp" and s[1] >= 2 and not spare[0]) or ((s[0] == "rt" or (s[0] == "mp" and s[1] < 2)) and not room["s"]):
                return None
            return max(t, clock[n], filled.get(s, 0))

        with tc.manual_schedule():
            while lists["v"] or lists["a"]:
                starts = [(start_of(n), i, n) for i, n in enumerate(("h", "s", "a", "v")) if start_of(n) is not None]
                assert starts, (lists["v"][:1], lists["a"][:1])
                t, i, n = min(starts)
                if n in rings:
                    s = rings[n].pop(0)
                    room[n].pop(0)
                    fills[s[0]][0](*s[1:])
                    clock["pe"] = t + fills[s[0]][2]
                    filled[s] = clock["pe"] + LATENCY
                else:
                    s = lists[n].pop(0)
                    steps[s[0]][0](*s[1:])
                    if s[0] == "mp" and s[1] < 2:
                        room["s"].pop(0)
                    elif s[0] == "mp":
                        spare[0] -= 1
                    elif s[0] == "mo" and s[1] >= 2:
                        spare[0] += 1
                    clock[n] = t + steps[s[0]][1]
                    done[s] = clock[n] + LATENCY
                    if s[0] == "mp":
                        clock["pe"] = max(clock["pe"] + 440, done[s] + 220)
                        done[s] = clock["pe"] + LATENCY
                    if s[0] == "rt":
                        room["s"].pop(0)
                    if s[0] == "rr" or (s[0] == "mo" and s[1] < 2):
                        room["s"].append(done[s])
                    if s[0] in fills:
                        room[fills[s[0]][1]].append(done[s])
